import numpy as np
import ml_dtypes


def mxq(x, axis, fmt="e4m3"):
    dtype, down = {"e4m3": (ml_dtypes.float8_e4m3fn, 7), "e5m2": (ml_dtypes.float8_e5m2, 14)}[fmt]
    v = np.moveaxis(np.asarray(x, np.float32).astype(ml_dtypes.bfloat16).astype(np.float64), axis, -1)
    blocks = v.reshape(v.shape[:-1] + (-1, 32))
    amax = np.abs(blocks).max(-1, keepdims=True)
    byte = np.maximum(np.where(amax > 0, np.frexp(amax)[1] - 1 + 127, 0) - down, 1)
    scale = np.exp2(byte - 127.0)
    codes = (blocks / scale).astype(np.float32).astype(dtype).astype(np.float64)
    return np.moveaxis((codes * scale).reshape(v.shape), -1, axis)


WIDE = False


def mx_kscale(k):
    if not WIDE:
        return np.ones(k)
    levels = np.array([10, -10, 5, -5, 0])
    if k % 512:
        return np.exp2(np.random.permutation(np.resize(levels, k // 32))).repeat(32)
    a = np.empty((k // 512, 16))
    for p in range(k // 512):
        a[p, :8] = np.random.permutation(np.resize(levels, 8))
        for g in range(8):
            far = levels[np.abs(levels - a[p, g]) >= 10]
            a[p, g + 8] = far[np.random.randint(len(far))]
    return np.exp2(a.ravel()).repeat(32)


def f64(x):
    return np.asarray(x).astype(np.float64)


def striped(idx):
    return np.tile(idx.reshape(-1, 16).T, (8, 1)).astype(np.uint16)


def unstriped(offs):
    return offs[:16].T.reshape(-1).astype(np.int64)


E2M1 = np.array([0.0, 0.5, 1.0, 1.5, 2.0, 3.0, 4.0, 6.0, -0.0, -0.5, -1.0, -1.5, -2.0, -3.0, -4.0, -6.0])


def pack_weight(w, fmt):
    k, n = w.shape
    w = f64(np.asarray(w, np.float32).astype(ml_dtypes.bfloat16)).reshape(k // 32, 32, n)
    amax = np.abs(w).max(1)
    if fmt == "e4m3":
        byte = np.frexp(amax)[1] - 1 + 127 - 7
    else:
        mant, ex = np.frexp(amax / 6.0)
        byte = np.where(mant > 0.5, ex, ex - 1) + 127
    byte = np.clip(np.where(amax > 0, byte, 1), 1, 254)
    scaled = (w * np.exp2(127.0 - byte)[:, None, :]).reshape(k, n).astype(np.float32)
    by_word = np.ascontiguousarray(scaled.reshape(k // 512, 128, 4, n).transpose(0, 1, 3, 2))
    if fmt == "e4m3":
        words = by_word.astype(ml_dtypes.float8_e4m3fn).view(np.uint8)
    else:
        c = by_word.astype(ml_dtypes.float4_e2m1fn).view(np.uint8) & 0xF
        words = (c[..., 0::2] | (c[..., 1::2] << 4)).reshape(k // 512, 128, 2 * n)
    return np.ascontiguousarray(words), np.ascontiguousarray(byte.astype(np.uint8).reshape(k // 512, 16, n))


def unpack_weight(words, scales, fmt):
    g, _, n = scales.shape
    words = np.ascontiguousarray(words).reshape(g, 128, n, -1)
    if fmt == "e4m3":
        vals = words.view(ml_dtypes.float8_e4m3fn).astype(np.float64)
    else:
        nib = np.empty((g, 128, n, 4), np.uint8)
        nib[..., 0::2] = words & 0xF
        nib[..., 1::2] = words >> 4
        vals = E2M1[nib]
    vals = vals * np.repeat(np.exp2(scales.astype(np.float64) - 127.0), 8, axis=1)[..., None]
    return vals.transpose(0, 1, 3, 2).reshape(g * 512, n)


def gelu(v):
    return 0.5 * v * (1.0 + np.tanh(np.sqrt(2.0 / np.pi) * (v + 0.044715 * v**3)))


K, K1, H, T, S, T2, P = 1536, 1024, 1024, 2048, 512, 1024, 512

def setup_inputs():
    n = np.random.standard_normal
    s = mx_kscale(K)[:, None]
    u = mx_kscale(H)[:, None]
    d = {}
    d["tab_words"], d["tab_scales"] = pack_weight(n((K, T)) * s, "e4m3")
    d["offs"] = striped(np.random.permutation(T)[:S])
    d["w1"] = (3.0 * n((K1, H)) / K**0.5 / s[:K1]).astype(np.float32)
    d["w4_words"], d["w4_scales"] = pack_weight(3.0 * n((K - K1, H)) / K**0.5 / s[K1:], "e2m1")
    d["mw"] = (0.75 * n((H, S)) * u).astype(np.float32)
    d["wgs"] = np.exp(0.3 * n((128, S))).astype(np.float32)
    d["page0"] = (n((H, T2)) * u).astype(np.float32)
    d["offs2"] = striped(np.random.permutation(T2)[:S])
    d["offs3"] = striped(np.random.permutation(T2)[:P])
    d["fl"] = (0.5 * n(H) * u[:, 0]).astype(np.float32)
    d["gv"] = (1.4 * n(H) / H**0.5 / u[:, 0]**2).astype(np.float32)
    d["bm"] = (0.7 * n((T2, P))).astype(np.float32)
    return d

def reference(tab_words, tab_scales, offs, w1, w4_words, w4_scales, mw, wgs, page0, offs2, offs3, fl, gv, bm):
    v = unpack_weight(tab_words, tab_scales, "e4m3")[:, unstriped(offs)]
    w1q = mxq(f64(w1), 0, "e4m3")
    w4 = unpack_weight(w4_words, w4_scales, "e2m1")
    f = w1q.T @ v[:K1] + w4.T @ v[K1:]
    h = np.log(1.0 + np.abs(f)) * f64(mw)
    page = f64(page0).copy()
    page[:, unstriped(offs2)] = np.tile(f64(wgs), (H // 128, 1)) * h
    x = np.maximum(page[:, unstriped(offs3)], f64(fl)[:, None]) * f64(gv)[:, None]
    e = mxq(page, 0, "e4m3").T @ mxq(x, 0, "e4m3")
    return np.tanh(e + f64(bm))

@@ -1,0 +1,316 @@
+from contextlib import ExitStack
+
+import concourse.mybir as mybir
+
+K, K1, H, T, S, T2, PN = 1536, 1024, 1024, 2048, 512, 1024, 512
+FLOPS = 2 * K * H * S + 2 * H * T2 * PN
+
+F32 = mybir.dt.float32
+BF16 = mybir.dt.bfloat16
+I32 = mybir.dt.int32
+U32 = mybir.dt.uint32
+U16 = mybir.dt.uint16
+U8 = mybir.dt.uint8
+FP8X4 = mybir.dt.float8_e4m3fn_x4
+FP4X4 = mybir.dt.float4_e2m1fn_x4
+ALU = mybir.AluOpType
+ACT = mybir.ActivationFunctionType
+
+P = 128
+PACK = 4
+KP = P * PACK
+
+
+def tile_list_wear_failure_scores_kernel(
+    tc, tab_words, tab_scales, offs, w1, w4_words, w4_scales, mw, wgs, page0, offs2, offs3, fl, gv, bm, out
+):
+    nc = tc.nc
+    with ExitStack() as ctx:
+        lists = ctx.enter_context(tc.tile_pool(name="lists", bufs=1))
+        keep = ctx.enter_context(tc.tile_pool(name="keep", bufs=1))
+        big = ctx.enter_context(tc.tile_pool(name="big", bufs=3))
+        weave = ctx.enter_context(tc.tile_pool(name="weave", bufs=4))
+        ring = ctx.enter_context(tc.tile_pool(name="ring", bufs=3))
+        psum = ctx.enter_context(tc.psum_pool(name="psum", bufs=1))
+
+        idx = lists.tile([P, S // 16], U16, name="idx")
+        idx2 = lists.tile([P, S // 16], U16, name="idx2")
+        idx3 = lists.tile([P, PN // 16], U16, name="idx3")
+
+        tab_sc = keep.tile([P, 3 * T], U8, name="tab_sc", align_bytes=64)
+        w4_sc_raw = keep.tile([P, H], U8, name="w4_sc_raw", align_bytes=64)
+        nc.vector.memset(tab_sc[:].bitcast(I32), 0)
+        nc.gpsimd.memset(w4_sc_raw[:].bitcast(I32), 0)
+
+        def load_w1(a, b):
+            raw = big.tile([P, PACK, KP], F32, name="big")
+            rows = w1[a * KP : (a + 1) * KP, b * KP : (b + 1) * KP]
+            nc.sync.dma_start(out=raw[:], in_=rows.rearrange("(p j) c -> p j c", j=PACK))
+            return raw
+
+        def load_tab(a):
+            words = keep.tile([P, T], I32, name="tab%d" % a, align_bytes=64)
+            nc.sync.dma_start(out=words[:], in_=tab_words[a].rearrange("p t i -> p (t i)").bitcast(I32))
+            return words
+
+        def rows_of(x, i):
+            b, t = divmod(i, PACK)
+            return x[b * KP : (b + 1) * KP, :].rearrange("(p t) c -> p t c", t=PACK)[:, t, :]
+
+        def load_page(i):
+            page = keep.tile([P, T2], F32, name="page%d" % i)
+            nc.sync.dma_start(out=page[:], in_=rows_of(page0, i))
+            return page
+
+        def load_mw(i):
+            tile = keep.tile([P, S], F32, name="mw%d" % i)
+            nc.sync.dma_start(out=tile[:], in_=rows_of(mw, i))
+            return tile
+
+        wgs_v = wgs.rearrange("(q t) j -> q t j", t=PACK)
+
+        w1_raw = {}
+        w1_raw[0, 0] = load_w1(0, 0)
+        nc.sync.dma_start(idx[:], offs)
+        for q in range(4):
+            nc.sync.dma_start(
+                out=tab_sc[32 * q : 32 * q + 4, :].bitcast(I32).rearrange("r (a t) -> r a t", a=3),
+                in_=tab_scales[:, 4 * q : 4 * q + 4, :].bitcast(I32).rearrange("a r t -> r a t"),
+            )
+        for q in range(4):
+            nc.gpsimd.dma_start(
+                out=w4_sc_raw[32 * q : 32 * q + 4, :].bitcast(I32),
+                in_=w4_scales[0, 4 * q : 4 * q + 4, :].bitcast(I32),
+            )
+        w1_raw[1, 0] = load_w1(1, 0)
+        w4_raw = keep.tile([P, 2 * H], U8, name="w4_raw", align_bytes=64)
+        nc.sync.dma_start(out=w4_raw[:].bitcast(I32), in_=w4_words[0].bitcast(I32))
+        tab = {}
+        for a in range(3):
+            tab[a] = load_tab(a)
+        wg0 = keep.tile([P, S], F32, name="wg0")
+        for q in (0, 2, 1, 3):
+            nc.sync.dma_start(out=wg0[32 * q : 32 * q + 32, :], in_=wgs_v[:, 0, :])
+        mws = {0: load_mw(0)}
+        pages = {0: load_page(0)}
+        nc.sync.dma_start(idx2[:], offs2)
+        nc.sync.dma_start(idx3[:], offs3)
+        wg123 = keep.tile([P, 3, S], F32, name="wg123")
+        mws[1] = load_mw(1)
+        for q in (0, 2, 1, 3):
+            nc.sync.dma_start(out=wg123[32 * q : 32 * q + 32, :, :], in_=wgs_v[:, 1:4, :])
+        pages[1] = load_page(1)
+        flv = keep.tile([P, 2, PACK], F32, name="flv")
+        gvv = keep.tile([P, 2, PACK], F32, name="gvv")
+        nc.sync.dma_start(out=flv[:], in_=fl.rearrange("(b p t) -> p b t", b=2, t=PACK))
+        nc.sync.dma_start(out=gvv[:], in_=gv.rearrange("(b p t) -> p b t", b=2, t=PACK))
+        w1_raw[0, 1] = load_w1(0, 1)
+        mws[2] = load_mw(2)
+        pages[2] = load_page(2)
+        w1_raw[1, 1] = load_w1(1, 1)
+        for i in range(3, 8):
+            mws[i] = load_mw(i)
+            pages[i] = load_page(i)
+        bms = []
+        for h in range(2):
+            tile = big.tile([P, PACK, PN], F32, name="big")
+            nc.sync.dma_start(out=tile[:], in_=bm[h * KP : (h + 1) * KP, :].rearrange("(u p) j -> p u j", p=P))
+            bms.append(tile)
+
+        v_s = {}
+        for a in range(3):
+            v_s[a] = keep.tile([P, S], U8, name="v_s%d" % a, align_bytes=64)
+            nc.vector.tensor_copy(v_s[a][:], tab_sc[:, a * T : (a + 1) * T].indirect(idx[:]))
+
+        w4_w = keep.tile([P, 2 * H], U8, name="w4_w", align_bytes=64)
+        w4_s = keep.tile([P, H], U8, name="w4_s", align_bytes=64)
+        nc.vector.tensor_copy(
+            out=w4_w[:].rearrange("p (b t m e) -> p b t m e", b=2, t=PACK, e=2),
+            in_=w4_raw[:].rearrange("p (b m t e) -> p b t m e", b=2, t=PACK, e=2),
+        )
+
+        def quantize(woven, name):
+            width = KP
+            codes = keep.tile([P, width], U32, name=name + "_c", align_bytes=64)
+            scales = keep.tile([P, width], U8, name=name + "_s", align_bytes=64)
+            nc.vector.quantize_mx(out=codes[:].bitcast(FP8X4), scales=scales[:], in_=woven[:])
+            return codes, scales
+
+        def weave_w1(a, b):
+            woven = weave.tile([P, PACK * KP], BF16, name="woven", align_bytes=64)
+            nc.scalar.copy(
+                out=woven[:].rearrange("p (t m j) -> p m j t", t=PACK, j=PACK),
+                in_=w1_raw[a, b][:].rearrange("p j (m t) -> p m j t", t=PACK),
+            )
+            return woven
+
+        def weave_planes(engine_copy, woven, planes, c0, c1, base):
+            engine_copy(
+                out=woven[:, PACK * c0 : PACK * c1].rearrange("p (c i t) -> p c t i", i=4, t=PACK),
+                in_=planes[:, :, base + c0 : base + c1].rearrange("p t (c i) -> p c t i", i=4),
+            )
+
+        w1_q = {}
+        for a in range(2):
+            w1_q[a, 0] = quantize(weave_w1(a, 0), "w1q%d0" % a)
+
+        v_w = {}
+        for a in range(3):
+            v_w[a] = keep.tile([P, S], U32, name="v_w%d" % a, align_bytes=64)
+            nc.vector.tensor_copy(v_w[a][:], tab[a][:].bitcast(U32).indirect(idx[:]))
+            if a == 0:
+                nc.vector.tensor_copy(
+                    out=w4_s[:].rearrange("p (b t m) -> p b t m", b=2, t=PACK),
+                    in_=w4_sc_raw[:].rearrange("p (b m t) -> p b t m", b=2, t=PACK),
+                )
+
+        logs = {}
+
+        def project(b):
+            banks = [psum.tile([P, S], F32, name="bank%d" % (PACK * b + t)) for t in range(PACK)]
+            for a in range(2):
+                codes, scales = w1_q[a, b]
+                for t in range(PACK):
+                    nc.tensor.matmul_mx(
+                        out=banks[t][:],
+                        lhsT=codes[:, t * P : (t + 1) * P].bitcast(FP8X4),
+                        lhsT_scale=scales[:, t * P : (t + 1) * P],
+                        rhs=v_w[a][:].bitcast(FP8X4),
+                        rhs_scale=v_s[a][:],
+                        start=(a == 0),
+                        stop=False,
+                    )
+            for t in range(PACK):
+                c0 = b * KP + t * P
+                nc.tensor.matmul_mx(
+                    out=banks[t][:],
+                    lhsT=w4_w[:, 2 * c0 : 2 * (c0 + P)].bitcast(FP4X4),
+                    lhsT_scale=w4_s[:, c0 : c0 + P],
+                    rhs=v_w[2][:].bitcast(FP8X4),
+                    rhs_scale=v_s[2][:],
+                    start=False,
+                    stop=True,
+                )
+            for t in range(PACK):
+                i = PACK * b + t
+                mag = ring.tile([P, S], F32, name="mag")
+                nc.scalar.activation(mag[:], banks[t][:], ACT.Abs)
+                logs[i] = keep.tile([P, S], F32, name="log%d" % i)
+                nc.scalar.activation(logs[i][:], mag[:], ACT.Ln, bias=1.0)
+
+        def premult(i):
+            t = i % PACK
+            wg = wg0[:] if t == 0 else wg123[:, t - 1, :]
+            nc.vector.tensor_tensor(mws[i][:], mws[i][:], wg, ALU.mult)
+
+        page_b = [keep.tile([P, PACK, T2], BF16, name="page_b%d" % b) for b in range(2)]
+        x_b = [keep.tile([P, PACK, PN], BF16, name="x_b%d" % b) for b in range(2)]
+        picked = {}
+
+        def scatter(i):
+            nc.vector.tensor_tensor(pages[i][:].indirect(idx2[:]), logs[i][:], mws[i][:], ALU.mult)
+
+        def cast_page(i):
+            b, t = divmod(i, PACK)
+            nc.scalar.copy(out=page_b[b][:, t, :], in_=pages[i][:])
+
+        def gather(i):
+            picked[i] = ring.tile([P, PN], F32, name="picked")
+            nc.vector.tensor_copy(picked[i][:], pages[i][:].indirect(idx3[:]))
+
+        def floor_weight(i):
+            b, t = divmod(i, PACK)
+            nc.vector.tensor_scalar(
+                x_b[b][:, t, :], picked[i][:], flv[:, b, t : t + 1], gvv[:, b, t : t + 1], ALU.max, ALU.mult
+            )
+
+        def weave_page(b, h):
+            woven = weave.tile([P, PACK * KP], BF16, name="woven", align_bytes=64)
+            weave_planes(nc.scalar.copy, woven, page_b[b], 0, KP, h * KP)
+            return woven
+
+        def weave_x(b, split):
+            woven = weave.tile([P, PACK * PN], BF16, name="woven", align_bytes=64)
+            if split > 0:
+                weave_planes(nc.vector.tensor_copy, woven, x_b[b], 0, split, 0)
+            if split < PN:
+                weave_planes(nc.scalar.copy, woven, x_b[b], split, PN, 0)
+            return woven
+
+        def score(b, banks, page_q, x_q):
+            for u in range(T2 // P):
+                codes, scales = page_q[u // PACK]
+                c0 = (u % PACK) * P
+                nc.tensor.matmul_mx(
+                    out=banks[u][:],
+                    lhsT=codes[:, c0 : c0 + P].bitcast(FP8X4),
+                    lhsT_scale=scales[:, c0 : c0 + P],
+                    rhs=x_q[0][:].bitcast(FP8X4),
+                    rhs_scale=x_q[1][:],
+                    start=(b == 0),
+                    stop=(b == 1),
+                )
+
+        premult(0)
+        project(0)
+        premult(1)
+        scatter(0)
+        cast_page(0)
+        premult(2)
+        gather(0)
+        woven_w = [weave_w1(0, 1)]
+        scatter(1)
+        cast_page(1)
+        floor_weight(0)
+        premult(3)
+        gather(1)
+        woven_w.append(weave_w1(1, 1))
+        scatter(2)
+        floor_weight(1)
+        for a in range(2):
+            w1_q[a, 1] = quantize(woven_w[a], "w1q%d1" % a)
+        project(1)
+        cast_page(2)
+        premult(4)
+        gather(2)
+        scatter(3)
+        cast_page(3)
+        floor_weight(2)
+        premult(5)
+        gather(3)
+        scatter(4)
+        floor_weight(3)
+        woven_p = [weave_page(0, h) for h in range(2)]
+        cast_page(4)
+        premult(6)
+        scatter(5)
+        woven_x = weave_x(0, 0)
+        cast_page(5)
+        premult(7)
+        page_q0 = [quantize(woven_p[h], "pq0%d" % h) for h in range(2)]
+        scatter(6)
+        cast_page(6)
+        x_q0 = quantize(woven_x, "xq0")
+        e_banks = [psum.tile([P, PN], F32, name="bank%d" % u) for u in range(T2 // P)]
+        score(0, e_banks, page_q0, x_q0)
+        scatter(7)
+        cast_page(7)
+        woven_p = [weave_page(1, h) for h in range(2)]
+        gather(4)
+        gather(5)
+        floor_weight(4)
+        gather(6)
+        floor_weight(5)
+        gather(7)
+        floor_weight(6)
+        page_q1 = [quantize(woven_p[0], "pq10")]
+        floor_weight(7)
+        woven_x = weave_x(1, PN)
+        page_q1.append(quantize(woven_p[1], "pq11"))
+        x_q1 = quantize(woven_x, "xq1")
+        score(1, e_banks, page_q1, x_q1)
+        for u in range(T2 // P):
+            rows = bms[u // PACK][:, u % PACK, :]
+            nc.vector.tensor_tensor(rows, e_banks[u][:], rows, ALU.add)
+            nc.scalar.activation(rows, rows, ACT.Tanh)
+            nc.sync.dma_start(out=out[u * P : (u + 1) * P, :], in_=rows)

@@ -2,7 +2,7 @@ from contextlib import ExitStack
 
 import concourse.mybir as mybir
 
-K, K1, H, T, S, T2, PN = 1536, 1024, 1024, 2048, 512, 1024, 512
+K, H, T, S, T2, PN = 1536, 1024, 2048, 512, 1024, 512
 FLOPS = 2 * K * H * S + 2 * H * T2 * PN
 
 F32 = mybir.dt.float32
@@ -19,6 +19,11 @@ ACT = mybir.ActivationFunctionType
 P = 128
 PACK = 4
 KP = P * PACK
+QUAD = 32
+ROW_TILES = H // P
+OUT_TILES = T2 // P
+QUADRANTS = (0, 2, 1, 3)
+X_WEAVE_ON_VECTOR = 192
 
 
 def tile_list_wear_failure_scores_kernel(
@@ -28,217 +33,235 @@ def tile_list_wear_failure_scores_kernel(
     with ExitStack() as ctx:
         lists = ctx.enter_context(tc.tile_pool(name="lists", bufs=1))
         keep = ctx.enter_context(tc.tile_pool(name="keep", bufs=1))
-        big = ctx.enter_context(tc.tile_pool(name="big", bufs=3))
-        weave = ctx.enter_context(tc.tile_pool(name="weave", bufs=4))
-        ring = ctx.enter_context(tc.tile_pool(name="ring", bufs=3))
+        slots = ctx.enter_context(tc.tile_pool(name="slots", bufs=1))
         psum = ctx.enter_context(tc.psum_pool(name="psum", bufs=1))
 
         idx = lists.tile([P, S // 16], U16, name="idx")
         idx2 = lists.tile([P, S // 16], U16, name="idx2")
         idx3 = lists.tile([P, PN // 16], U16, name="idx3")
 
-        tab_sc = keep.tile([P, 3 * T], U8, name="tab_sc", align_bytes=64)
+        tab_sc = keep.tile([P, T], U8, name="tab_sc", align_bytes=64)
+        tab_sc_in = keep.tile([P, T // 4], I32, name="tab_sc_in", align_bytes=64)
         w4_sc_raw = keep.tile([P, H], U8, name="w4_sc_raw", align_bytes=64)
         nc.vector.memset(tab_sc[:].bitcast(I32), 0)
         nc.gpsimd.memset(w4_sc_raw[:].bitcast(I32), 0)
 
+        warm = keep.tile([P, 1], F32, name="warm")
+        warm_out = keep.tile([P, 2], F32, name="warm_out")
+        nc.vector.memset(warm[:], 1.0)
+        nc.scalar.activation(warm_out[:, 0:1], warm[:], ACT.Ln, bias=1.0)
+
+        def load_scale_rows(q):
+            rows = tab_scales[:, 4 * q : 4 * q + 4, :].bitcast(I32)
+            nc.sync.dma_start(out=tab_sc_in[QUAD * q : QUAD * q + 4, :], in_=rows[2])
+            nc.sync.dma_start(out=tab_sc_in[QUAD * q + 4 : QUAD * q + 12, :], in_=rows[0:2])
+
         def load_w1(a, b):
-            raw = big.tile([P, PACK, KP], F32, name="big")
+            raw = slots.tile([P, PACK, KP], F32, name="w1_raw%d%d" % (a, b), align_bytes=64)
             rows = w1[a * KP : (a + 1) * KP, b * KP : (b + 1) * KP]
             nc.sync.dma_start(out=raw[:], in_=rows.rearrange("(p j) c -> p j c", j=PACK))
             return raw
 
         def load_tab(a):
-            words = keep.tile([P, T], I32, name="tab%d" % a, align_bytes=64)
+            words = slots.tile([P, T], I32, name="tab%d" % a, align_bytes=64)
             nc.sync.dma_start(out=words[:], in_=tab_words[a].rearrange("p t i -> p (t i)").bitcast(I32))
             return words
 
-        def rows_of(x, i):
+        def row_tile(matrix, i):
             b, t = divmod(i, PACK)
-            return x[b * KP : (b + 1) * KP, :].rearrange("(p t) c -> p t c", t=PACK)[:, t, :]
+            return matrix[b * KP : (b + 1) * KP, :].rearrange("(p t) c -> p t c", t=PACK)[:, t, :]
 
         def load_page(i):
             page = keep.tile([P, T2], F32, name="page%d" % i)
-            nc.sync.dma_start(out=page[:], in_=rows_of(page0, i))
+            nc.sync.dma_start(out=page[:], in_=row_tile(page0, i))
             return page
 
         def load_mw(i):
-            tile = keep.tile([P, S], F32, name="mw%d" % i)
-            nc.sync.dma_start(out=tile[:], in_=rows_of(mw, i))
-            return tile
+            weight = slots.tile([P, S], F32, name="mw%d" % i, align_bytes=64)
+            nc.sync.dma_start(out=weight[:], in_=row_tile(mw, i))
+            return weight
 
-        wgs_v = wgs.rearrange("(q t) j -> q t j", t=PACK)
+        wgs_rows = wgs.rearrange("(q t) j -> q t j", t=PACK)
 
-        w1_raw = {}
+        w1_raw, tab, weights, pages = {}, {}, {}, {}
+        load_scale_rows(0)
+        load_scale_rows(2)
         w1_raw[0, 0] = load_w1(0, 0)
-        nc.sync.dma_start(idx[:], offs)
-        for q in range(4):
-            nc.sync.dma_start(
-                out=tab_sc[32 * q : 32 * q + 4, :].bitcast(I32).rearrange("r (a t) -> r a t", a=3),
-                in_=tab_scales[:, 4 * q : 4 * q + 4, :].bitcast(I32).rearrange("a r t -> r a t"),
-            )
-        for q in range(4):
-            nc.gpsimd.dma_start(
-                out=w4_sc_raw[32 * q : 32 * q + 4, :].bitcast(I32),
-                in_=w4_scales[0, 4 * q : 4 * q + 4, :].bitcast(I32),
-            )
-        w1_raw[1, 0] = load_w1(1, 0)
         w4_raw = keep.tile([P, 2 * H], U8, name="w4_raw", align_bytes=64)
         nc.sync.dma_start(out=w4_raw[:].bitcast(I32), in_=w4_words[0].bitcast(I32))
-        tab = {}
+        w1_raw[1, 0] = load_w1(1, 0)
+        nc.sync.dma_start(idx[:], offs)
+        load_scale_rows(1)
+        load_scale_rows(3)
+        for q in range(4):
+            nc.gpsimd.dma_start(
+                out=w4_sc_raw[QUAD * q : QUAD * q + 4, :].bitcast(I32),
+                in_=w4_scales[0, 4 * q : 4 * q + 4, :].bitcast(I32),
+            )
         for a in range(3):
             tab[a] = load_tab(a)
-        wg0 = keep.tile([P, S], F32, name="wg0")
-        for q in (0, 2, 1, 3):
-            nc.sync.dma_start(out=wg0[32 * q : 32 * q + 32, :], in_=wgs_v[:, 0, :])
-        mws = {0: load_mw(0)}
-        pages = {0: load_page(0)}
         nc.sync.dma_start(idx2[:], offs2)
+        weights[0] = load_mw(0)
+        wgs_first = keep.tile([P, S], F32, name="wgs_first")
+        for q in QUADRANTS:
+            nc.sync.dma_start(out=wgs_first[QUAD * q : QUAD * (q + 1), :], in_=wgs_rows[:, 0, :])
+        pages[0] = load_page(0)
         nc.sync.dma_start(idx3[:], offs3)
-        wg123 = keep.tile([P, 3, S], F32, name="wg123")
-        mws[1] = load_mw(1)
-        for q in (0, 2, 1, 3):
-            nc.sync.dma_start(out=wg123[32 * q : 32 * q + 32, :, :], in_=wgs_v[:, 1:4, :])
+        wgs_rest = keep.tile([P, PACK - 1, S], F32, name="wgs_rest")
+        weights[1] = load_mw(1)
+        weights[2] = load_mw(2)
+        for q in QUADRANTS:
+            nc.sync.dma_start(out=wgs_rest[QUAD * q : QUAD * (q + 1), :, :], in_=wgs_rows[:, 1:PACK, :])
         pages[1] = load_page(1)
-        flv = keep.tile([P, 2, PACK], F32, name="flv")
-        gvv = keep.tile([P, 2, PACK], F32, name="gvv")
-        nc.sync.dma_start(out=flv[:], in_=fl.rearrange("(b p t) -> p b t", b=2, t=PACK))
-        nc.sync.dma_start(out=gvv[:], in_=gv.rearrange("(b p t) -> p b t", b=2, t=PACK))
+        floor = keep.tile([P, 2, PACK], F32, name="floor")
+        gain = keep.tile([P, 2, PACK], F32, name="gain")
+        nc.sync.dma_start(out=floor[:], in_=fl.rearrange("(b p t) -> p b t", b=2, t=PACK))
+        nc.sync.dma_start(out=gain[:], in_=gv.rearrange("(b p t) -> p b t", b=2, t=PACK))
         w1_raw[0, 1] = load_w1(0, 1)
-        mws[2] = load_mw(2)
+        weights[3] = load_mw(3)
         pages[2] = load_page(2)
         w1_raw[1, 1] = load_w1(1, 1)
-        for i in range(3, 8):
-            mws[i] = load_mw(i)
+        for i in range(PACK, ROW_TILES - 1):
+            weights[i] = load_mw(i)
+        pages[3] = load_page(3)
+        weights[ROW_TILES - 1] = load_mw(ROW_TILES - 1)
+        for i in range(PACK, ROW_TILES):
             pages[i] = load_page(i)
-        bms = []
+        bm_tiles = []
         for h in range(2):
-            tile = big.tile([P, PACK, PN], F32, name="big")
-            nc.sync.dma_start(out=tile[:], in_=bm[h * KP : (h + 1) * KP, :].rearrange("(u p) j -> p u j", p=P))
-            bms.append(tile)
+            bias = slots.tile([P, PACK, PN], F32, name="w1_raw%d0" % h, align_bytes=64)
+            nc.sync.dma_start(out=bias[:], in_=bm[h * KP : (h + 1) * KP, :].rearrange("(u p) j -> p u j", p=P))
+            bm_tiles.append(bias)
 
-        v_s = {}
-        for a in range(3):
-            v_s[a] = keep.tile([P, S], U8, name="v_s%d" % a, align_bytes=64)
-            nc.vector.tensor_copy(v_s[a][:], tab_sc[:, a * T : (a + 1) * T].indirect(idx[:]))
+        for q in QUADRANTS:
+            rows = slice(QUAD * q, QUAD * q + 12)
+            nc.vector.tensor_copy(tab_sc[rows, :].bitcast(I32), tab_sc_in[rows, :])
+        v_sc = keep.tile([P, S], U8, name="v_sc", align_bytes=64)
+        nc.vector.tensor_copy(v_sc[:], tab_sc[:].indirect(idx[:]))
+        v_scales = {0: v_sc[4:P, :], 1: v_sc[8:P, :], 2: v_sc[:]}
 
-        w4_w = keep.tile([P, 2 * H], U8, name="w4_w", align_bytes=64)
-        w4_s = keep.tile([P, H], U8, name="w4_s", align_bytes=64)
+        w4_codes = keep.tile([P, 2 * H], U8, name="w4_codes", align_bytes=64)
         nc.vector.tensor_copy(
-            out=w4_w[:].rearrange("p (b t m e) -> p b t m e", b=2, t=PACK, e=2),
+            out=w4_codes[:].rearrange("p (b t m e) -> p b t m e", b=2, t=PACK, e=2),
             in_=w4_raw[:].rearrange("p (b m t e) -> p b t m e", b=2, t=PACK, e=2),
         )
 
         def quantize(woven, name):
-            width = KP
-            codes = keep.tile([P, width], U32, name=name + "_c", align_bytes=64)
-            scales = keep.tile([P, width], U8, name=name + "_s", align_bytes=64)
+            codes = slots.tile([P, KP], U32, name=name + "_codes", align_bytes=64)
+            scales = keep.tile([P, KP], U8, name=name + "_scales", align_bytes=64)
             nc.vector.quantize_mx(out=codes[:].bitcast(FP8X4), scales=scales[:], in_=woven[:])
             return codes, scales
 
         def weave_w1(a, b):
-            woven = weave.tile([P, PACK * KP], BF16, name="woven", align_bytes=64)
+            woven = slots.tile([P, PACK * KP], BF16, name=("woven%d", "mag%d")[b] % a, align_bytes=64)
             nc.scalar.copy(
                 out=woven[:].rearrange("p (t m j) -> p m j t", t=PACK, j=PACK),
                 in_=w1_raw[a, b][:].rearrange("p j (m t) -> p m j t", t=PACK),
             )
             return woven
 
-        def weave_planes(engine_copy, woven, planes, c0, c1, base):
-            engine_copy(
+        def weave_rows(copy, woven, rows, c0, c1, base):
+            copy(
                 out=woven[:, PACK * c0 : PACK * c1].rearrange("p (c i t) -> p c t i", i=4, t=PACK),
-                in_=planes[:, :, base + c0 : base + c1].rearrange("p t (c i) -> p c t i", i=4),
+                in_=rows[:, :, base + c0 : base + c1].rearrange("p t (c i) -> p c t i", i=4),
             )
 
         w1_q = {}
         for a in range(2):
             w1_q[a, 0] = quantize(weave_w1(a, 0), "w1q%d0" % a)
 
-        v_w = {}
-        for a in range(3):
-            v_w[a] = keep.tile([P, S], U32, name="v_w%d" % a, align_bytes=64)
-            nc.vector.tensor_copy(v_w[a][:], tab[a][:].bitcast(U32).indirect(idx[:]))
-            if a == 0:
-                nc.vector.tensor_copy(
-                    out=w4_s[:].rearrange("p (b t m) -> p b t m", b=2, t=PACK),
-                    in_=w4_sc_raw[:].rearrange("p (b m t) -> p b t m", b=2, t=PACK),
-                )
+        v_codes = {}
+
+        def gather_words(a):
+            v_codes[a] = keep.tile([P, S], U32, name="v_codes%d" % a, align_bytes=64)
+            nc.vector.tensor_copy(v_codes[a][:], tab[a][:].bitcast(U32).indirect(idx[:]))
+
+        gather_words(0)
+        gather_words(1)
+        w4_sc = slots.tile([P, H], U8, name="tab1", align_bytes=64)
+        nc.vector.tensor_copy(
+            out=w4_sc[:].rearrange("p (b t m) -> p b t m", b=2, t=PACK),
+            in_=w4_sc_raw[:].rearrange("p (b m t) -> p b t m", b=2, t=PACK),
+        )
+        gather_words(2)
 
         logs = {}
 
-        def project(b):
-            banks = [psum.tile([P, S], F32, name="bank%d" % (PACK * b + t)) for t in range(PACK)]
-            for a in range(2):
-                codes, scales = w1_q[a, b]
-                for t in range(PACK):
+        def project(b, group):
+            banks = {}
+            for t in group:
+                banks[t] = psum.tile([P, S], F32, name="bank%d" % (t % 2 if b == 0 else PACK + t))
+            for a in range(3):
+                for t in group:
+                    if a < 2:
+                        codes, scales = w1_q[a, b]
+                        lhs = codes[:, t * P : (t + 1) * P].bitcast(FP8X4)
+                        lhs_scale = scales[:, t * P : (t + 1) * P]
+                    else:
+                        c0 = b * KP + t * P
+                        lhs = w4_codes[:, 2 * c0 : 2 * (c0 + P)].bitcast(FP4X4)
+                        lhs_scale = w4_sc[:, c0 : c0 + P]
                     nc.tensor.matmul_mx(
                         out=banks[t][:],
-                        lhsT=codes[:, t * P : (t + 1) * P].bitcast(FP8X4),
-                        lhsT_scale=scales[:, t * P : (t + 1) * P],
-                        rhs=v_w[a][:].bitcast(FP8X4),
-                        rhs_scale=v_s[a][:],
+                        lhsT=lhs,
+                        lhsT_scale=lhs_scale,
+                        rhs=v_codes[a][:].bitcast(FP8X4),
+                        rhs_scale=v_scales[a],
                         start=(a == 0),
-                        stop=False,
+                        stop=(a == 2),
                     )
-            for t in range(PACK):
-                c0 = b * KP + t * P
-                nc.tensor.matmul_mx(
-                    out=banks[t][:],
-                    lhsT=w4_w[:, 2 * c0 : 2 * (c0 + P)].bitcast(FP4X4),
-                    lhsT_scale=w4_s[:, c0 : c0 + P],
-                    rhs=v_w[2][:].bitcast(FP8X4),
-                    rhs_scale=v_s[2][:],
-                    start=False,
-                    stop=True,
-                )
-            for t in range(PACK):
+            for t in group:
                 i = PACK * b + t
-                mag = ring.tile([P, S], F32, name="mag")
+                mag = slots.tile([P, S], F32, name="mag%d" % (t % 2 if b == 0 else 2 + t), align_bytes=64)
                 nc.scalar.activation(mag[:], banks[t][:], ACT.Abs)
-                logs[i] = keep.tile([P, S], F32, name="log%d" % i)
+                logs[i] = slots.tile([P, S], F32, name="log%d" % i, align_bytes=64)
                 nc.scalar.activation(logs[i][:], mag[:], ACT.Ln, bias=1.0)
 
-        def premult(i):
+        def weigh(i):
             t = i % PACK
-            wg = wg0[:] if t == 0 else wg123[:, t - 1, :]
-            nc.vector.tensor_tensor(mws[i][:], mws[i][:], wg, ALU.mult)
+            factor = wgs_first[:] if t == 0 else wgs_rest[:, t - 1, :]
+            nc.vector.tensor_tensor(weights[i][:], weights[i][:], factor, ALU.mult)
 
-        page_b = [keep.tile([P, PACK, T2], BF16, name="page_b%d" % b) for b in range(2)]
-        x_b = [keep.tile([P, PACK, PN], BF16, name="x_b%d" % b) for b in range(2)]
-        picked = {}
+        page_bf, x_bf, picked = {}, {}, {}
 
         def scatter(i):
-            nc.vector.tensor_tensor(pages[i][:].indirect(idx2[:]), logs[i][:], mws[i][:], ALU.mult)
+            nc.vector.tensor_tensor(pages[i][:].indirect(idx2[:]), logs[i][:], weights[i][:], ALU.mult)
 
-        def cast_page(i):
+        def round_page(i):
             b, t = divmod(i, PACK)
-            nc.scalar.copy(out=page_b[b][:, t, :], in_=pages[i][:])
+            if t == 0:
+                page_bf[b] = slots.tile([P, PACK, T2], BF16, name="w1_raw%d1" % (1 - b), align_bytes=64)
+            nc.scalar.copy(out=page_bf[b][:, t, :], in_=pages[i][:])
 
-        def gather(i):
-            picked[i] = ring.tile([P, PN], F32, name="picked")
-            nc.vector.tensor_copy(picked[i][:], pages[i][:].indirect(idx3[:]))
+        def gather(i, into):
+            picked[i] = into
+            nc.vector.tensor_copy(into, pages[i][:].indirect(idx3[:]))
 
-        def floor_weight(i):
+        def picks(slot, count):
+            return slots.tile([P, count, PN], F32, name=slot, align_bytes=64)
+
+        def floor_and_gain(i):
             b, t = divmod(i, PACK)
+            if t == 0:
+                x_bf[b] = slots.tile([P, PACK, PN], BF16, name=("mag5", "x_bf1")[b], align_bytes=64)
             nc.vector.tensor_scalar(
-                x_b[b][:, t, :], picked[i][:], flv[:, b, t : t + 1], gvv[:, b, t : t + 1], ALU.max, ALU.mult
+                x_bf[b][:, t, :], picked[i], floor[:, b, t : t + 1], gain[:, b, t : t + 1], ALU.max, ALU.mult
             )
 
         def weave_page(b, h):
-            woven = weave.tile([P, PACK * KP], BF16, name="woven", align_bytes=64)
-            weave_planes(nc.scalar.copy, woven, page_b[b], 0, KP, h * KP)
+            woven = slots.tile([P, PACK * KP], BF16, name="woven%d" % h, align_bytes=64)
+            weave_rows(nc.scalar.copy, woven, page_bf[b], 0, KP, h * KP)
             return woven
 
-        def weave_x(b, split):
-            woven = weave.tile([P, PACK * PN], BF16, name="woven", align_bytes=64)
-            if split > 0:
-                weave_planes(nc.vector.tensor_copy, woven, x_b[b], 0, split, 0)
-            if split < PN:
-                weave_planes(nc.scalar.copy, woven, x_b[b], split, PN, 0)
+        def weave_x(b, on_vector):
+            woven = slots.tile([P, PACK * PN], BF16, name="woven%d" % (2 + b), align_bytes=64)
+            if on_vector > 0:
+                weave_rows(nc.vector.tensor_copy, woven, x_bf[b], 0, on_vector, 0)
+            weave_rows(nc.scalar.copy, woven, x_bf[b], on_vector, PN, 0)
             return woven
 
         def score(b, banks, page_q, x_q):
-            for u in range(T2 // P):
+            for u in range(OUT_TILES):
                 codes, scales = page_q[u // PACK]
                 c0 = (u % PACK) * P
                 nc.tensor.matmul_mx(
@@ -251,66 +274,71 @@ def tile_list_wear_failure_scores_kernel(
                     stop=(b == 1),
                 )
 
-        premult(0)
-        project(0)
-        premult(1)
+        weigh(0)
+        for group in ((0, 1), (2,), (3,)):
+            project(0, group)
         scatter(0)
-        cast_page(0)
-        premult(2)
-        gather(0)
-        woven_w = [weave_w1(0, 1)]
+        gather(0, picks("picked0", 1)[:, 0, :])
+        weigh(1)
+        weigh(2)
         scatter(1)
-        cast_page(1)
-        floor_weight(0)
-        premult(3)
-        gather(1)
-        woven_w.append(weave_w1(1, 1))
+        gather(1, picks("picked1", 1)[:, 0, :])
+        weigh(3)
         scatter(2)
-        floor_weight(1)
         for a in range(2):
-            w1_q[a, 1] = quantize(woven_w[a], "w1q%d1" % a)
-        project(1)
-        cast_page(2)
-        premult(4)
-        gather(2)
+            w1_q[a, 1] = quantize(weave_w1(a, 1), "w1q%d1" % a)
+        round_page(0)
+        round_page(1)
+        for t in range(PACK):
+            project(1, (t,))
+        nc.scalar.activation(warm_out[:, 1:2], logs[ROW_TILES - 1][:, 0:1], ACT.Tanh)
+        round_page(2)
+        for i in range(PACK, ROW_TILES):
+            weigh(i)
         scatter(3)
-        cast_page(3)
-        floor_weight(2)
-        premult(5)
-        gather(3)
+        round_page(3)
+
+        woven_page = [weave_page(0, h) for h in range(2)]
         scatter(4)
-        floor_weight(3)
-        woven_p = [weave_page(0, h) for h in range(2)]
-        cast_page(4)
-        premult(6)
+        round_page(4)
+        gather(2, picks("mag2", 1)[:, 0, :])
         scatter(5)
-        woven_x = weave_x(0, 0)
-        cast_page(5)
-        premult(7)
-        page_q0 = [quantize(woven_p[h], "pq0%d" % h) for h in range(2)]
+        round_page(5)
+        gather(3, picks("mag3", 1)[:, 0, :])
         scatter(6)
-        cast_page(6)
-        x_q0 = quantize(woven_x, "xq0")
-        e_banks = [psum.tile([P, PN], F32, name="bank%d" % u) for u in range(T2 // P)]
-        score(0, e_banks, page_q0, x_q0)
+        for i in range(PACK):
+            floor_and_gain(i)
+        woven_x = weave_x(0, 0)
+        round_page(6)
         scatter(7)
-        cast_page(7)
-        woven_p = [weave_page(1, h) for h in range(2)]
-        gather(4)
-        gather(5)
-        floor_weight(4)
-        gather(6)
-        floor_weight(5)
-        gather(7)
-        floor_weight(6)
-        page_q1 = [quantize(woven_p[0], "pq10")]
-        floor_weight(7)
-        woven_x = weave_x(1, PN)
-        page_q1.append(quantize(woven_p[1], "pq11"))
+        round_page(7)
+
+        page_q0 = [quantize(woven_page[h], "pq0%d" % h) for h in range(2)]
+        woven_page = [weave_page(1, h) for h in range(2)]
+        pair = picks("w1_raw11", 2)
+        gather(4, pair[:, 0, :])
+        gather(5, pair[:, 1, :])
+        floor_and_gain(4)
+        floor_and_gain(5)
+        x_q0 = quantize(woven_x, "xq0")
+        e_banks = [psum.tile([P, PN], F32, name="bank%d" % u) for u in range(OUT_TILES)]
+        score(0, e_banks, page_q0, x_q0)
+        pair = picks("mag5", 2)
+        gather(6, pair[:, 0, :])
+        gather(7, pair[:, 1, :])
+        floor_and_gain(6)
+        floor_and_gain(7)
+        page_q1 = [quantize(woven_page[0], "pq10")]
+        woven_x = weave_x(1, X_WEAVE_ON_VECTOR)
+        page_q1.append(quantize(woven_page[1], "pq11"))
         x_q1 = quantize(woven_x, "xq1")
         score(1, e_banks, page_q1, x_q1)
-        for u in range(T2 // P):
-            rows = bms[u // PACK][:, u % PACK, :]
-            nc.vector.tensor_tensor(rows, e_banks[u][:], rows, ALU.add)
-            nc.scalar.activation(rows, rows, ACT.Tanh)
-            nc.sync.dma_start(out=out[u * P : (u + 1) * P, :], in_=rows)
+
+        for u in range(OUT_TILES):
+            parts = 2 if u == OUT_TILES - 1 else 1
+            for part in range(parts):
+                cols = slice(part * PN // parts, (part + 1) * PN // parts)
+                result = bm_tiles[u // PACK][:, u % PACK, cols]
+                nc.vector.tensor_tensor(result, e_banks[u][:, cols], result, ALU.add)
+                nc.scalar.activation(result, result, ACT.Tanh)
+                nc.sync.dma_start(out=out[u * P : (u + 1) * P, cols], in_=result)

from contextlib import ExitStack

import concourse.mybir as mybir

K, H, T, S, T2, PN = 1536, 1024, 2048, 512, 1024, 512
FLOPS = 2 * K * H * S + 2 * H * T2 * PN

F32 = mybir.dt.float32
BF16 = mybir.dt.bfloat16
I32 = mybir.dt.int32
U32 = mybir.dt.uint32
U16 = mybir.dt.uint16
U8 = mybir.dt.uint8
FP8X4 = mybir.dt.float8_e4m3fn_x4
FP4X4 = mybir.dt.float4_e2m1fn_x4
ALU = mybir.AluOpType
ACT = mybir.ActivationFunctionType

P = 128
PACK = 4
KP = P * PACK
QUAD = 32
ROW_TILES = H // P
OUT_TILES = T2 // P
QUADRANTS = (0, 2, 1, 3)
X_WEAVE_ON_VECTOR = 192


def tile_list_wear_failure_scores_kernel(
    tc, tab_words, tab_scales, offs, w1, w4_words, w4_scales, mw, wgs, page0, offs2, offs3, fl, gv, bm, out
):
    nc = tc.nc
    with ExitStack() as ctx:
        lists = ctx.enter_context(tc.tile_pool(name="lists", bufs=1))
        keep = ctx.enter_context(tc.tile_pool(name="keep", bufs=1))
        slots = ctx.enter_context(tc.tile_pool(name="slots", bufs=1))
        psum = ctx.enter_context(tc.psum_pool(name="psum", bufs=1))

        idx = lists.tile([P, S // 16], U16, name="idx")
        idx2 = lists.tile([P, S // 16], U16, name="idx2")
        idx3 = lists.tile([P, PN // 16], U16, name="idx3")

        tab_sc = keep.tile([P, T], U8, name="tab_sc", align_bytes=64)
        tab_sc_in = keep.tile([P, T // 4], I32, name="tab_sc_in", align_bytes=64)
        w4_sc_raw = keep.tile([P, H], U8, name="w4_sc_raw", align_bytes=64)
        nc.vector.memset(tab_sc[:].bitcast(I32), 0)
        nc.gpsimd.memset(w4_sc_raw[:].bitcast(I32), 0)

        warm = keep.tile([P, 1], F32, name="warm")
        warm_out = keep.tile([P, 2], F32, name="warm_out")
        nc.vector.memset(warm[:], 1.0)
        nc.scalar.activation(warm_out[:, 0:1], warm[:], ACT.Ln, bias=1.0)

        def load_scale_rows(q):
            rows = tab_scales[:, 4 * q : 4 * q + 4, :].bitcast(I32)
            nc.sync.dma_start(out=tab_sc_in[QUAD * q : QUAD * q + 4, :], in_=rows[2])
            nc.sync.dma_start(out=tab_sc_in[QUAD * q + 4 : QUAD * q + 12, :], in_=rows[0:2])

        def load_w1(a, b):
            raw = slots.tile([P, PACK, KP], F32, name="w1_raw%d%d" % (a, b), align_bytes=64)
            rows = w1[a * KP : (a + 1) * KP, b * KP : (b + 1) * KP]
            nc.sync.dma_start(out=raw[:], in_=rows.rearrange("(p j) c -> p j c", j=PACK))
            return raw

        def load_tab(a):
            words = slots.tile([P, T], I32, name="tab%d" % a, align_bytes=64)
            nc.sync.dma_start(out=words[:], in_=tab_words[a].rearrange("p t i -> p (t i)").bitcast(I32))
            return words

        def row_tile(matrix, i):
            b, t = divmod(i, PACK)
            return matrix[b * KP : (b + 1) * KP, :].rearrange("(p t) c -> p t c", t=PACK)[:, t, :]

        def load_page(i):
            page = keep.tile([P, T2], F32, name="page%d" % i)
            nc.sync.dma_start(out=page[:], in_=row_tile(page0, i))
            return page

        def load_mw(i):
            weight = slots.tile([P, S], F32, name="mw%d" % i, align_bytes=64)
            nc.sync.dma_start(out=weight[:], in_=row_tile(mw, i))
            return weight

        wgs_rows = wgs.rearrange("(q t) j -> q t j", t=PACK)

        w1_raw, tab, weights, pages = {}, {}, {}, {}
        load_scale_rows(0)
        load_scale_rows(2)
        w1_raw[0, 0] = load_w1(0, 0)
        w4_raw = keep.tile([P, 2 * H], U8, name="w4_raw", align_bytes=64)
        nc.sync.dma_start(out=w4_raw[:].bitcast(I32), in_=w4_words[0].bitcast(I32))
        w1_raw[1, 0] = load_w1(1, 0)
        nc.sync.dma_start(idx[:], offs)
        load_scale_rows(1)
        load_scale_rows(3)
        for q in range(4):
            nc.gpsimd.dma_start(
                out=w4_sc_raw[QUAD * q : QUAD * q + 4, :].bitcast(I32),
                in_=w4_scales[0, 4 * q : 4 * q + 4, :].bitcast(I32),
            )
        for a in range(3):
            tab[a] = load_tab(a)
        nc.sync.dma_start(idx2[:], offs2)
        weights[0] = load_mw(0)
        wgs_first = keep.tile([P, S], F32, name="wgs_first")
        for q in QUADRANTS:
            nc.sync.dma_start(out=wgs_first[QUAD * q : QUAD * (q + 1), :], in_=wgs_rows[:, 0, :])
        pages[0] = load_page(0)
        nc.sync.dma_start(idx3[:], offs3)
        wgs_rest = keep.tile([P, PACK - 1, S], F32, name="wgs_rest")
        weights[1] = load_mw(1)
        weights[2] = load_mw(2)
        for q in QUADRANTS:
            nc.sync.dma_start(out=wgs_rest[QUAD * q : QUAD * (q + 1), :, :], in_=wgs_rows[:, 1:PACK, :])
        pages[1] = load_page(1)
        floor = keep.tile([P, 2, PACK], F32, name="floor")
        gain = keep.tile([P, 2, PACK], F32, name="gain")
        nc.sync.dma_start(out=floor[:], in_=fl.rearrange("(b p t) -> p b t", b=2, t=PACK))
        nc.sync.dma_start(out=gain[:], in_=gv.rearrange("(b p t) -> p b t", b=2, t=PACK))
        w1_raw[0, 1] = load_w1(0, 1)
        weights[3] = load_mw(3)
        pages[2] = load_page(2)
        w1_raw[1, 1] = load_w1(1, 1)
        for i in range(PACK, ROW_TILES - 1):
            weights[i] = load_mw(i)
        pages[3] = load_page(3)
        weights[ROW_TILES - 1] = load_mw(ROW_TILES - 1)
        for i in range(PACK, ROW_TILES):
            pages[i] = load_page(i)
        bm_tiles = []
        for h in range(2):
            bias = slots.tile([P, PACK, PN], F32, name="w1_raw%d0" % h, align_bytes=64)
            nc.sync.dma_start(out=bias[:], in_=bm[h * KP : (h + 1) * KP, :].rearrange("(u p) j -> p u j", p=P))
            bm_tiles.append(bias)

        for q in QUADRANTS:
            rows = slice(QUAD * q, QUAD * q + 12)
            nc.vector.tensor_copy(tab_sc[rows, :].bitcast(I32), tab_sc_in[rows, :])
        v_sc = keep.tile([P, S], U8, name="v_sc", align_bytes=64)
        nc.vector.tensor_copy(v_sc[:], tab_sc[:].indirect(idx[:]))
        v_scales = {0: v_sc[4:P, :], 1: v_sc[8:P, :], 2: v_sc[:]}

        w4_codes = keep.tile([P, 2 * H], U8, name="w4_codes", align_bytes=64)
        nc.vector.tensor_copy(
            out=w4_codes[:].rearrange("p (b t m e) -> p b t m e", b=2, t=PACK, e=2),
            in_=w4_raw[:].rearrange("p (b m t e) -> p b t m e", b=2, t=PACK, e=2),
        )

        def quantize(woven, name):
            codes = slots.tile([P, KP], U32, name=name + "_codes", align_bytes=64)
            scales = keep.tile([P, KP], U8, name=name + "_scales", align_bytes=64)
            nc.vector.quantize_mx(out=codes[:].bitcast(FP8X4), scales=scales[:], in_=woven[:])
            return codes, scales

        def weave_w1(a, b):
            woven = slots.tile([P, PACK * KP], BF16, name=("woven%d", "mag%d")[b] % a, align_bytes=64)
            nc.scalar.copy(
                out=woven[:].rearrange("p (t m j) -> p m j t", t=PACK, j=PACK),
                in_=w1_raw[a, b][:].rearrange("p j (m t) -> p m j t", t=PACK),
            )
            return woven

        def weave_rows(copy, woven, rows, c0, c1, base):
            copy(
                out=woven[:, PACK * c0 : PACK * c1].rearrange("p (c i t) -> p c t i", i=4, t=PACK),
                in_=rows[:, :, base + c0 : base + c1].rearrange("p t (c i) -> p c t i", i=4),
            )

        w1_q = {}
        for a in range(2):
            w1_q[a, 0] = quantize(weave_w1(a, 0), "w1q%d0" % a)

        v_codes = {}

        def gather_words(a):
            v_codes[a] = keep.tile([P, S], U32, name="v_codes%d" % a, align_bytes=64)
            nc.vector.tensor_copy(v_codes[a][:], tab[a][:].bitcast(U32).indirect(idx[:]))

        gather_words(0)
        gather_words(1)
        w4_sc = slots.tile([P, H], U8, name="tab1", align_bytes=64)
        nc.vector.tensor_copy(
            out=w4_sc[:].rearrange("p (b t m) -> p b t m", b=2, t=PACK),
            in_=w4_sc_raw[:].rearrange("p (b m t) -> p b t m", b=2, t=PACK),
        )
        gather_words(2)

        logs = {}

        def project(b, group):
            banks = {}
            for t in group:
                banks[t] = psum.tile([P, S], F32, name="bank%d" % (t % 2 if b == 0 else PACK + t))
            for a in range(3):
                for t in group:
                    if a < 2:
                        codes, scales = w1_q[a, b]
                        lhs = codes[:, t * P : (t + 1) * P].bitcast(FP8X4)
                        lhs_scale = scales[:, t * P : (t + 1) * P]
                    else:
                        c0 = b * KP + t * P
                        lhs = w4_codes[:, 2 * c0 : 2 * (c0 + P)].bitcast(FP4X4)
                        lhs_scale = w4_sc[:, c0 : c0 + P]
                    nc.tensor.matmul_mx(
                        out=banks[t][:],
                        lhsT=lhs,
                        lhsT_scale=lhs_scale,
                        rhs=v_codes[a][:].bitcast(FP8X4),
                        rhs_scale=v_scales[a],
                        start=(a == 0),
                        stop=(a == 2),
                    )
            for t in group:
                i = PACK * b + t
                mag = slots.tile([P, S], F32, name="mag%d" % (t % 2 if b == 0 else 2 + t), align_bytes=64)
                nc.scalar.activation(mag[:], banks[t][:], ACT.Abs)
                logs[i] = slots.tile([P, S], F32, name="log%d" % i, align_bytes=64)
                nc.scalar.activation(logs[i][:], mag[:], ACT.Ln, bias=1.0)

        def weigh(i):
            t = i % PACK
            factor = wgs_first[:] if t == 0 else wgs_rest[:, t - 1, :]
            nc.vector.tensor_tensor(weights[i][:], weights[i][:], factor, ALU.mult)

        page_bf, x_bf, picked = {}, {}, {}

        def scatter(i):
            nc.vector.tensor_tensor(pages[i][:].indirect(idx2[:]), logs[i][:], weights[i][:], ALU.mult)

        def round_page(i):
            b, t = divmod(i, PACK)
            if t == 0:
                page_bf[b] = slots.tile([P, PACK, T2], BF16, name="w1_raw%d1" % (1 - b), align_bytes=64)
            nc.scalar.copy(out=page_bf[b][:, t, :], in_=pages[i][:])

        def gather(i, into):
            picked[i] = into
            nc.vector.tensor_copy(into, pages[i][:].indirect(idx3[:]))

        def picks(slot, count):
            return slots.tile([P, count, PN], F32, name=slot, align_bytes=64)

        def floor_and_gain(i):
            b, t = divmod(i, PACK)
            if t == 0:
                x_bf[b] = slots.tile([P, PACK, PN], BF16, name=("mag5", "x_bf1")[b], align_bytes=64)
            nc.vector.tensor_scalar(
                x_bf[b][:, t, :], picked[i], floor[:, b, t : t + 1], gain[:, b, t : t + 1], ALU.max, ALU.mult
            )

        def weave_page(b, h):
            woven = slots.tile([P, PACK * KP], BF16, name="woven%d" % h, align_bytes=64)
            weave_rows(nc.scalar.copy, woven, page_bf[b], 0, KP, h * KP)
            return woven

        def weave_x(b, on_vector):
            woven = slots.tile([P, PACK * PN], BF16, name="woven%d" % (2 + b), align_bytes=64)
            if on_vector > 0:
                weave_rows(nc.vector.tensor_copy, woven, x_bf[b], 0, on_vector, 0)
            weave_rows(nc.scalar.copy, woven, x_bf[b], on_vector, PN, 0)
            return woven

        def score(b, banks, page_q, x_q):
            for u in range(OUT_TILES):
                codes, scales = page_q[u // PACK]
                c0 = (u % PACK) * P
                nc.tensor.matmul_mx(
                    out=banks[u][:],
                    lhsT=codes[:, c0 : c0 + P].bitcast(FP8X4),
                    lhsT_scale=scales[:, c0 : c0 + P],
                    rhs=x_q[0][:].bitcast(FP8X4),
                    rhs_scale=x_q[1][:],
                    start=(b == 0),
                    stop=(b == 1),
                )

        weigh(0)
        for group in ((0, 1), (2,), (3,)):
            project(0, group)
        scatter(0)
        gather(0, picks("picked0", 1)[:, 0, :])
        weigh(1)
        weigh(2)
        scatter(1)
        gather(1, picks("picked1", 1)[:, 0, :])
        weigh(3)
        scatter(2)
        for a in range(2):
            w1_q[a, 1] = quantize(weave_w1(a, 1), "w1q%d1" % a)
        round_page(0)
        round_page(1)
        for t in range(PACK):
            project(1, (t,))
        nc.scalar.activation(warm_out[:, 1:2], logs[ROW_TILES - 1][:, 0:1], ACT.Tanh)
        round_page(2)
        for i in range(PACK, ROW_TILES):
            weigh(i)
        scatter(3)
        round_page(3)

        woven_page = [weave_page(0, h) for h in range(2)]
        scatter(4)
        round_page(4)
        gather(2, picks("mag2", 1)[:, 0, :])
        scatter(5)
        round_page(5)
        gather(3, picks("mag3", 1)[:, 0, :])
        scatter(6)
        for i in range(PACK):
            floor_and_gain(i)
        woven_x = weave_x(0, 0)
        round_page(6)
        scatter(7)
        round_page(7)

        page_q0 = [quantize(woven_page[h], "pq0%d" % h) for h in range(2)]
        woven_page = [weave_page(1, h) for h in range(2)]
        pair = picks("w1_raw11", 2)
        gather(4, pair[:, 0, :])
        gather(5, pair[:, 1, :])
        floor_and_gain(4)
        floor_and_gain(5)
        x_q0 = quantize(woven_x, "xq0")
        e_banks = [psum.tile([P, PN], F32, name="bank%d" % u) for u in range(OUT_TILES)]
        score(0, e_banks, page_q0, x_q0)
        pair = picks("mag5", 2)
        gather(6, pair[:, 0, :])
        gather(7, pair[:, 1, :])
        floor_and_gain(6)
        floor_and_gain(7)
        page_q1 = [quantize(woven_page[0], "pq10")]
        woven_x = weave_x(1, X_WEAVE_ON_VECTOR)
        page_q1.append(quantize(woven_page[1], "pq11"))
        x_q1 = quantize(woven_x, "xq1")
        score(1, e_banks, page_q1, x_q1)

        for u in range(OUT_TILES):
            parts = 2 if u == OUT_TILES - 1 else 1
            for part in range(parts):
                cols = slice(part * PN // parts, (part + 1) * PN // parts)
                result = bm_tiles[u // PACK][:, u % PACK, cols]
                nc.vector.tensor_tensor(result, e_banks[u][:, cols], result, ALU.add)
                nc.scalar.activation(result, result, ACT.Tanh)
                nc.sync.dma_start(out=out[u * P : (u + 1) * P, cols], in_=result)
